import numpy as np
import ml_dtypes


def mxq(x, axis, fmt="e4m3"):
    dtype, down = {"e4m3": (ml_dtypes.float8_e4m3fn, 7), "e5m2": (ml_dtypes.float8_e5m2, 14)}[fmt]
    v = np.moveaxis(np.asarray(x, np.float32).astype(ml_dtypes.bfloat16).astype(np.float64), axis, -1)
    blocks = v.reshape(v.shape[:-1] + (-1, 32))
    amax = np.abs(blocks).max(-1, keepdims=True)
    byte = np.maximum(np.where(amax > 0, np.frexp(amax)[1] - 1 + 127, 0) - down, 1)
    scale = np.exp2(byte - 127.0)
    codes = (blocks / scale).astype(np.float32).astype(dtype).astype(np.float64)
    return np.moveaxis((codes * scale).reshape(v.shape), -1, axis)


WIDE = False


def mx_kscale(k):
    if not WIDE:
        return np.ones(k)
    levels = np.array([10, -10, 5, -5, 0])
    if k % 512:
        return np.exp2(np.random.permutation(np.resize(levels, k // 32))).repeat(32)
    a = np.empty((k // 512, 16))
    for p in range(k // 512):
        a[p, :8] = np.random.permutation(np.resize(levels, 8))
        for g in range(8):
            far = levels[np.abs(levels - a[p, g]) >= 10]
            a[p, g + 8] = far[np.random.randint(len(far))]
    return np.exp2(a.ravel()).repeat(32)


def f64(x):
    return np.asarray(x).astype(np.float64)


def striped(idx):
    return np.tile(idx.reshape(-1, 16).T, (8, 1)).astype(np.uint16)


def unstriped(offs):
    return offs[:16].T.reshape(-1).astype(np.int64)


def striped8(idx):
    return np.concatenate([x.reshape(-1, 16).T for x in idx]).astype(np.uint16)


def runs(offs, k):
    lists = np.stack([offs[16 * r : 16 * r + 16].T.reshape(-1) for r in range(8)]).astype(np.int64)
    return lists[np.arange(k) % 512 // 64]


def pack_weight(w):
    k, n = w.shape
    w = f64(np.asarray(w, np.float32).astype(ml_dtypes.bfloat16)).reshape(k // 32, 32, n)
    amax = np.abs(w).max(1)
    byte = np.clip(np.where(amax > 0, np.frexp(amax)[1] - 1 + 127 - 7, 1), 1, 254)
    scaled = (w * np.exp2(127.0 - byte)[:, None, :]).reshape(k, n).astype(np.float32)
    words = np.ascontiguousarray(scaled.reshape(k // 512, 128, 4, n).transpose(0, 1, 3, 2)).astype(ml_dtypes.float8_e4m3fn).view(np.uint8)
    return words, np.ascontiguousarray(byte.astype(np.uint8).reshape(k // 512, 16, n))


def unpack_weight(words, scales):
    g, p, n, _ = words.shape
    vals = np.ascontiguousarray(words).view(ml_dtypes.float8_e4m3fn).astype(np.float64) * np.repeat(np.exp2(scales.astype(np.float64) - 127.0), 8, axis=1)[..., None]
    return vals.transpose(0, 1, 3, 2).reshape(g * 512, n)


def sigmoid(v):
    return 1.0 / (1.0 + np.exp(-np.maximum(v, -700.0)))


K, T, S, N, H, W = 512, 2048, 512, 512, 512, 2048


def setup_inputs():
    n = np.random.standard_normal
    s = mx_kscale(K)[:, None]
    u = mx_kscale(H)
    packed_xT = pack_weight(n((K, T)) * s)
    return {
        "x_words": packed_xT[0],
        "x_scales": packed_xT[1],
        "w1": (n((K, H)) / np.sqrt(K) / s).astype(np.float32),
        "w2": (n((K, H)) / np.sqrt(K) / s).astype(np.float32),
        "gn": (np.random.uniform(0.5, 1.5, (H, 1)) * u[:, None]).astype(np.float32),
        "w3": (n((H, N)) / np.sqrt(H) / u[:, None]).astype(np.float32),
        "offs": striped(np.random.permutation(T)[:S]),
        "hz": striped8(np.random.randint(0, T, (8, S))),
        "n1": striped8(np.stack([np.random.permutation(S) for _ in range(8)])),
        "n2": striped8(np.stack([np.random.permutation(S) for _ in range(8)])),
        "n3": striped(np.random.randint(0, S, W)),
    }


def reference(x_words, x_scales, w1, w2, gn, w3, offs, hz, n1, n2, n3):
    xq = unpack_weight(x_words, x_scales)[:, unstriped(offs)]
    y = mxq(f64(w1), 0, "e4m3").T @ xq
    x_hz = unpack_weight(x_words, x_scales)[np.arange(K)[:, None], runs(hz, K)]
    d = mxq(f64(w2), 0, "e4m3").T @ x_hz
    z = f64(gn) * ((y + y[np.arange(H)[:, None], runs(n1, H)]) * (sigmoid(d + d[np.arange(H)[:, None], runs(n2, H)])))
    h = mxq(f64(w3), 0, "e4m3").T @ mxq(z, 0, "e4m3")
    mb = h[:, unstriped(n3)]
    mx = mb.reshape(N, S, 4).max(axis=2)
    mn = mb.reshape(N, S, 4).min(axis=2)
    return mx - (0.5 * mn)

@@ -1,0 +1,230 @@
+from contextlib import ExitStack
+
+import concourse.mybir as mybir
+
+K, T, S, N, H, W = 512, 2048, 512, 512, 512, 2048
+FLOPS = 2 * (K * H * S * 2 + H * N * S)
+
+F32 = mybir.dt.float32
+BF16 = mybir.dt.bfloat16
+I32 = mybir.dt.int32
+U32 = mybir.dt.uint32
+U16 = mybir.dt.uint16
+U8 = mybir.dt.uint8
+FP8X4 = mybir.dt.float8_e4m3fn_x4
+ALU = mybir.AluOpType
+ACT = mybir.ActivationFunctionType
+
+P = 128
+PACK = 4
+HALF = S // 2
+MEMBERS = 4
+SPARE = 16
+GATHER = 512
+
+
+def tile_picked_twhtriebgspan_none_p_kernel(
+    tc, x_words, x_scales, w1, w2, gn, w3, offs, hz, n1, n2, n3, out
+):
+    nc = tc.nc
+    with ExitStack() as ctx:
+        keep = ctx.enter_context(tc.tile_pool(name="keep", bufs=1))
+        raws = ctx.enter_context(tc.tile_pool(name="raws", bufs=4))
+        work = ctx.enter_context(tc.tile_pool(name="work", bufs=2))
+        pool3 = ctx.enter_context(tc.tile_pool(name="pool3", bufs=4))
+        psum = ctx.enter_context(tc.psum_pool(name="psum", bufs=8))
+
+        offs_t = keep.tile([P, S // 16], U16, name="offs_t")
+        hz_t = keep.tile([P, S // 16], U16, name="hz_t")
+        n1_t = keep.tile([P, S // 16], U16, name="n1_t")
+        n2_t = keep.tile([P, S // 16], U16, name="n2_t")
+        n3_t = keep.tile([P, W // 16], U16, name="n3_t")
+        word_table = keep.tile([P, T], U32, name="word_table")
+        byte_table = keep.tile([P, T], U8, name="byte_table")
+        gain = keep.tile([P, PACK], F32, name="gain")
+        h_rows = [keep.tile([P, S + SPARE], F32, name="h_rows%d" % n) for n in range(N // P)]
+
+        nc.vector.memset(byte_table[:].bitcast(I32), 0)
+        for n in range(N // P):
+            nc.gpsimd.memset(h_rows[n][:, S:], 0.0)
+
+        def load_weight(w):
+            raw = raws.tile([P, PACK, w.shape[1]], F32, name="raw", align_bytes=64)
+            nc.sync.dma_start(raw[:], w.rearrange("(p j) c -> p j c", j=PACK))
+            return raw
+
+        nc.sync.dma_start(offs_t[:], offs)
+        nc.scalar.dma_start(gain[:], gn.rearrange("(p t) o -> p (t o)", t=PACK))
+        nc.scalar.dma_start(byte_table[0:P:8, :].bitcast(I32), x_scales[0].bitcast(I32))
+        for r in range(1, 4):
+            nc.scalar.dma_start(byte_table[r:P:32, :].bitcast(I32), x_scales[0][r:16:4, :].bitcast(I32))
+        w1_raw = [load_weight(w1[:, c : c + H // 2]) for c in (0, H // 2)]
+        nc.sync.dma_start(hz_t[:], hz)
+        nc.sync.dma_start(word_table[:].bitcast(I32), x_words[0].rearrange("p n t -> p (n t)").bitcast(I32))
+        w2_raw = load_weight(w2)
+
+        x_bytes = keep.tile([P, S], U8, name="x_bytes", align_bytes=64)
+        nc.vector.tensor_copy(x_bytes[:], byte_table[:].indirect(offs_t[:]))
+        hz_picked = keep.tile([P, S], U8, name="hz_picked", align_bytes=64)
+        nc.vector.tensor_copy(hz_picked[:], byte_table[:].indirect(hz_t[:]))
+        hz_bytes = keep.tile([P, S], U8, name="hz_bytes", align_bytes=64)
+        nc.vector.tensor_copy(hz_bytes[:].bitcast(I32), hz_picked[:].bitcast(I32))
+        for r in (2, 3):
+            nc.sync.dma_start(hz_bytes[r:P:32, :].bitcast(I32), hz_picked[8 * r : P : 32, :].bitcast(I32))
+        nc.sync.dma_start(n1_t[:], n1)
+        nc.sync.dma_start(n2_t[:], n2)
+        nc.sync.dma_start(n3_t[:], n3)
+        w3_raw = load_weight(w3)
+
+        def dealt_views(grouped, raw):
+            return grouped.rearrange("p t m j -> p m j t"), raw[:].rearrange("p j (m t) -> p m j t", t=PACK)
+
+        def quantise(name, grouped, width):
+            codes = keep.tile([P, width], U32, name=name + "_codes", align_bytes=64)
+            scales = keep.tile([P, width], U8, name=name + "_scales", align_bytes=64)
+            nc.vector.quantize_mx(out=codes[:].bitcast(FP8X4), scales=scales[:], in_=grouped)
+            return codes, scales
+
+        def product(weights, block, codes, scales, width):
+            acc = psum.tile([P, width], F32, name="acc")
+            cols = slice(block * P, (block + 1) * P)
+            nc.tensor.matmul_mx(
+                out=acc[:],
+                lhsT=weights[0][:, cols].bitcast(FP8X4),
+                lhsT_scale=weights[1][:, cols],
+                rhs=codes.bitcast(FP8X4),
+                rhs_scale=scales,
+                start=True,
+                stop=True,
+            )
+            return acc
+
+        w1_dealt = keep.tile([P, PACK, P, PACK], BF16, name="dealt", align_bytes=64)
+        for i in range(2):
+            dst, src = dealt_views(w1_dealt[:, :, i * P // 2 : (i + 1) * P // 2, :], w1_raw[i])
+            nc.scalar.activation(dst, src, ACT.Copy)
+        w1_q = quantise("w1", w1_dealt[:].rearrange("p t m j -> p (t m j)"), H)
+        x_codes = keep.tile([P, S], U32, name="x_codes", align_bytes=64)
+        nc.vector.tensor_copy(x_codes[:], word_table[:].indirect(offs_t[:]))
+
+        y_rows = []
+        for t in range(PACK):
+            acc = product(w1_q, t, x_codes[:], x_bytes[:], S)
+            row = keep.tile([P, S], F32, name="y_rows%d" % t)
+            nc.scalar.activation(row[:], acc[:], ACT.Copy, scale=gain[:, t : t + 1])
+            y_rows.append(row)
+
+        hz_codes = raws.tile([P, S], U32, name="raw", align_bytes=64)
+        nc.vector.tensor_copy(hz_codes[:], word_table[:].indirect(hz_t[:]))
+        w2_dealt = keep.tile([P, PACK, P, PACK], BF16, name="dealt", align_bytes=64)
+        dst, src = dealt_views(w2_dealt[:], w2_raw)
+        nc.vector.tensor_copy(dst, src)
+        w2_q = quantise("w2", w2_dealt[:].rearrange("p t m j -> p (t m j)"), H)
+
+        d_rows = []
+        for t in range(PACK):
+            acc = product(w2_q, t, hz_codes[:], hz_bytes[:], S)
+            row = keep.tile([P, S], F32, name="d_rows%d" % t)
+            nc.scalar.copy(row[:], acc[:])
+            d_rows.append(row)
+
+        def fetch(on_vector, dst, looked_up):
+            if on_vector:
+                nc.vector.tensor_copy(dst, looked_up)
+            else:
+                nc.scalar.activation(dst, looked_up, ACT.Copy)
+
+        y_sums = []
+        for half in range(2):
+            cols = slice(half * HALF, (half + 1) * HALF)
+            lcols = slice(half * HALF // 16, (half + 1) * HALF // 16)
+            y_near = work.tile([P, PACK, HALF], F32, name="y_near")
+            y_sum = work.tile([P, PACK, HALF], F32, name="y_sum")
+            for t in range(PACK):
+                fetch(half == 1, y_near[:, t, :], y_rows[t][:].indirect(n1_t[:, lcols]))
+            for t in range(PACK):
+                nc.vector.tensor_tensor(y_sum[:, t, :], y_near[:, t, :], y_rows[t][:, cols], ALU.add)
+            y_sums.append(y_sum)
+
+        def quantise_w3(n, grouped):
+            nc.scalar.copy(
+                grouped.rearrange("p (c i) j -> p c j i", i=4),
+                w3_raw[:, :, n * P : (n + 1) * P].rearrange("p j (c i) -> p c j i", i=4),
+            )
+            return quantise("w3_%d" % n, grouped.rearrange("p n j -> p (n j)"), P)
+
+        w3_first = keep.tile([P, P, PACK], BF16, name="w3_first", align_bytes=64)
+        z_codes = keep.tile([P, S], U32, name="z_codes", align_bytes=64)
+        z_scales = keep.tile([P, S], U8, name="z_scales", align_bytes=64)
+        for half in range(2):
+            cols = slice(half * HALF, (half + 1) * HALF)
+            lcols = slice(half * HALF // 16, (half + 1) * HALF // 16)
+            d_near = work.tile([P, PACK, HALF], F32, name="d_near")
+            d_sum = keep.tile([P, PACK, HALF], F32, name="d_sum%d" % half, align_bytes=64)
+            gate = work.tile([P, PACK, HALF], F32, name="gate")
+            for t in range(PACK):
+                fetch(half == 0 and t < 2, d_near[:, t, :], d_rows[t][:].indirect(n2_t[:, lcols]))
+            for t in range(PACK):
+                nc.vector.tensor_tensor(d_sum[:, t, :], d_near[:, t, :], d_rows[t][:, cols], ALU.add)
+            for pair in range(2):
+                ts = slice(2 * pair, 2 * pair + 2)
+                nc.scalar.activation(gate[:, ts, :], d_sum[:, ts, :], ACT.Sigmoid)
+            z = work.tile([P, HALF, PACK], BF16, name="z", align_bytes=64)
+            nc.vector.tensor_tensor(
+                z[:].rearrange("p (c i) t -> p c t i", i=2),
+                y_sums[half][:].rearrange("p t (c i) -> p c t i", i=2),
+                gate[:].rearrange("p t (c i) -> p c t i", i=2),
+                ALU.mult,
+            )
+            nc.vector.quantize_mx(
+                out=z_codes[:, cols].bitcast(FP8X4), scales=z_scales[:, cols], in_=z[:].rearrange("p c t -> p (c t)")
+            )
+            if half == 0:
+                w3_q = quantise_w3(0, w3_first[:])
+            acc = product(w3_q, 0, z_codes[:, cols], z_scales[:, cols], HALF)
+            nc.scalar.copy(h_rows[0][:, cols], acc[:])
+
+        w3_rest = keep.tile([P, N - P, PACK], BF16, name="d_sum1", align_bytes=64)
+        for n in range(1, N // P):
+            w3_q = quantise_w3(n, w3_rest[:, (n - 1) * P : n * P, :])
+            acc = product(w3_q, 0, z_codes[:], z_scales[:], S)
+            nc.vector.tensor_copy(h_rows[n][:, :S], acc[:])
+
+        chunks = []
+        for n in range(N // P):
+            widths = [1024, 1024] if n < N // P - 1 else [1024, 512, 512]
+            start = 0
+            for width in widths:
+                chunks.append((n, start, width))
+                start = start + width
+
+        def finish(n, start, width, largest, smallest):
+            places = width // MEMBERS
+            result = pool3.tile([P, places], F32, name="result")
+            nc.vector.scalar_tensor_tensor(result[:], smallest[:], -0.5, largest[:], ALU.mult, ALU.add)
+            first = start // MEMBERS
+            nc.sync.dma_start(out[n * P : (n + 1) * P, first : first + places], result[:])
+
+        pending = None
+        for n, start, width in chunks:
+            places = width // MEMBERS
+            members = pool3.tile([P, width], F32, name="members")
+            for s in range(0, width, GATHER):
+                looked_up = h_rows[n][:].indirect(n3_t[:, (start + s) // 16 : (start + s + GATHER) // 16])
+                if n == 0 and start + s == GATHER:
+                    nc.vector.tensor_copy(members[:, s : s + GATHER], looked_up)
+                else:
+                    nc.scalar.activation(members[:, s : s + GATHER], looked_up, ACT.Copy)
+            by_place = members[:].rearrange("p (j m) -> p j m", m=MEMBERS)
+            high = work.tile([P, places, 2], F32, name="high")
+            low = work.tile([P, places, 2], F32, name="low")
+            nc.vector.tensor_tensor(high[:], by_place[:, :, 0:2], by_place[:, :, 2:4], ALU.max)
+            nc.vector.tensor_tensor(low[:], by_place[:, :, 0:2], by_place[:, :, 2:4], ALU.min)
+            if pending is not None:
+                finish(*pending)
+            largest = work.tile([P, places], F32, name="largest")
+            smallest = work.tile([P, places], F32, name="smallest")
+            nc.vector.tensor_tensor(largest[:], high[:, :, 0], high[:, :, 1], ALU.max)
+            nc.vector.tensor_tensor(smallest[:], low[:, :, 0], low[:, :, 1], ALU.min)
+            pending = (n, start, width, largest, smallest)
+        finish(*pending)

@@ -29,10 +29,9 @@ def tile_picked_twhtriebgspan_none_p_kernel(
     nc = tc.nc
     with ExitStack() as ctx:
         keep = ctx.enter_context(tc.tile_pool(name="keep", bufs=1))
-        raws = ctx.enter_context(tc.tile_pool(name="raws", bufs=4))
         work = ctx.enter_context(tc.tile_pool(name="work", bufs=2))
         pool3 = ctx.enter_context(tc.tile_pool(name="pool3", bufs=4))
-        psum = ctx.enter_context(tc.psum_pool(name="psum", bufs=8))
+        psum = ctx.enter_context(tc.psum_pool(name="psum", bufs=1))
 
         offs_t = keep.tile([P, S // 16], U16, name="offs_t")
         hz_t = keep.tile([P, S // 16], U16, name="hz_t")
@@ -48,20 +47,22 @@ def tile_picked_twhtriebgspan_none_p_kernel(
         for n in range(N // P):
             nc.gpsimd.memset(h_rows[n][:, S:], 0.0)
 
-        def load_weight(w):
-            raw = raws.tile([P, PACK, w.shape[1]], F32, name="raw", align_bytes=64)
+        def load_weight(name, w):
+            raw = keep.tile([P, PACK, w.shape[1]], F32, name=name)
             nc.sync.dma_start(raw[:], w.rearrange("(p j) c -> p j c", j=PACK))
             return raw
 
         nc.sync.dma_start(offs_t[:], offs)
-        nc.scalar.dma_start(gain[:], gn.rearrange("(p t) o -> p (t o)", t=PACK))
-        nc.scalar.dma_start(byte_table[0:P:8, :].bitcast(I32), x_scales[0].bitcast(I32))
-        for r in range(1, 4):
-            nc.scalar.dma_start(byte_table[r:P:32, :].bitcast(I32), x_scales[0][r:16:4, :].bitcast(I32))
-        w1_raw = [load_weight(w1[:, c : c + H // 2]) for c in (0, H // 2)]
         nc.sync.dma_start(hz_t[:], hz)
+        nc.sync.dma_start(byte_table[0:P:8, :].bitcast(I32), x_scales[0].bitcast(I32))
+        for r in range(1, 4):
+            nc.sync.dma_start(byte_table[r:P:32, :].bitcast(I32), x_scales[0][r:16:4, :].bitcast(I32))
+        nc.scalar.dma_start(gain[:], gn.rearrange("(p t) o -> p (t o)", t=PACK))
+        warm = keep.tile([P, 1], F32, name="warm")
+        nc.scalar.activation(warm[:], gain[:, 0:1], ACT.Sigmoid)
         nc.sync.dma_start(word_table[:].bitcast(I32), x_words[0].rearrange("p n t -> p (n t)").bitcast(I32))
-        w2_raw = load_weight(w2)
+        w1_raw = [load_weight("w1_raw%d" % i, w1[:, i * H // 2 : (i + 1) * H // 2]) for i in range(2)]
+        w2_raw = [load_weight("w2_raw%d" % i, w2[:, i * H // 2 : (i + 1) * H // 2]) for i in range(2)]
 
         x_bytes = keep.tile([P, S], U8, name="x_bytes", align_bytes=64)
         nc.vector.tensor_copy(x_bytes[:], byte_table[:].indirect(offs_t[:]))
@@ -73,8 +74,8 @@ def tile_picked_twhtriebgspan_none_p_kernel(
             nc.sync.dma_start(hz_bytes[r:P:32, :].bitcast(I32), hz_picked[8 * r : P : 32, :].bitcast(I32))
         nc.sync.dma_start(n1_t[:], n1)
         nc.sync.dma_start(n2_t[:], n2)
+        w3_raw = load_weight("w3_raw", w3)
         nc.sync.dma_start(n3_t[:], n3)
-        w3_raw = load_weight(w3)
 
         def dealt_views(grouped, raw):
             return grouped.rearrange("p t m j -> p m j t"), raw[:].rearrange("p j (m t) -> p m j t", t=PACK)
@@ -85,8 +86,8 @@ def tile_picked_twhtriebgspan_none_p_kernel(
             nc.vector.quantize_mx(out=codes[:].bitcast(FP8X4), scales=scales[:], in_=grouped)
             return codes, scales
 
-        def product(weights, block, codes, scales, width):
-            acc = psum.tile([P, width], F32, name="acc")
+        def product(weights, block, codes, scales, width, bank):
+            acc = psum.tile([P, width], F32, name=bank)
             cols = slice(block * P, (block + 1) * P)
             nc.tensor.matmul_mx(
                 out=acc[:],
@@ -99,31 +100,30 @@ def tile_picked_twhtriebgspan_none_p_kernel(
             )
             return acc
 
-        w1_dealt = keep.tile([P, PACK, P, PACK], BF16, name="dealt", align_bytes=64)
+        w1_dealt = keep.tile([P, PACK, P, PACK], BF16, name="w1_dealt", align_bytes=64)
+        w2_dealt = keep.tile([P, PACK, P, PACK], BF16, name="w2_dealt", align_bytes=64)
         for i in range(2):
-            dst, src = dealt_views(w1_dealt[:, :, i * P // 2 : (i + 1) * P // 2, :], w1_raw[i])
-            nc.scalar.activation(dst, src, ACT.Copy)
-        w1_q = quantise("w1", w1_dealt[:].rearrange("p t m j -> p (t m j)"), H)
+            nc.scalar.copy(*dealt_views(w1_dealt[:, :, i * P // 2 : (i + 1) * P // 2, :], w1_raw[i]))
         x_codes = keep.tile([P, S], U32, name="x_codes", align_bytes=64)
         nc.vector.tensor_copy(x_codes[:], word_table[:].indirect(offs_t[:]))
+        hz_codes = keep.tile([P, S], U32, name="hz_codes", align_bytes=64)
+        nc.vector.tensor_copy(hz_codes[:], word_table[:].indirect(hz_t[:]))
+        w1_q = quantise("w1", w1_dealt[:].rearrange("p t m j -> p (t m j)"), H)
+        nc.scalar.copy(*dealt_views(w2_dealt[:, :, : P // 2, :], w2_raw[0]))
 
         y_rows = []
         for t in range(PACK):
-            acc = product(w1_q, t, x_codes[:], x_bytes[:], S)
+            acc = product(w1_q, t, x_codes[:], x_bytes[:], S, "bank%d" % t)
             row = keep.tile([P, S], F32, name="y_rows%d" % t)
             nc.scalar.activation(row[:], acc[:], ACT.Copy, scale=gain[:, t : t + 1])
             y_rows.append(row)
 
-        hz_codes = raws.tile([P, S], U32, name="raw", align_bytes=64)
-        nc.vector.tensor_copy(hz_codes[:], word_table[:].indirect(hz_t[:]))
-        w2_dealt = keep.tile([P, PACK, P, PACK], BF16, name="dealt", align_bytes=64)
-        dst, src = dealt_views(w2_dealt[:], w2_raw)
-        nc.vector.tensor_copy(dst, src)
+        nc.vector.tensor_copy(*dealt_views(w2_dealt[:, :, P // 2 :, :], w2_raw[1]))
         w2_q = quantise("w2", w2_dealt[:].rearrange("p t m j -> p (t m j)"), H)
 
         d_rows = []
         for t in range(PACK):
-            acc = product(w2_q, t, hz_codes[:], hz_bytes[:], S)
+            acc = product(w2_q, t, hz_codes[:], hz_bytes[:], S, "bank%d" % (PACK + t))
             row = keep.tile([P, S], F32, name="d_rows%d" % t)
             nc.scalar.copy(row[:], acc[:])
             d_rows.append(row)
@@ -141,7 +141,7 @@ def tile_picked_twhtriebgspan_none_p_kernel(
             y_near = work.tile([P, PACK, HALF], F32, name="y_near")
             y_sum = work.tile([P, PACK, HALF], F32, name="y_sum")
             for t in range(PACK):
-                fetch(half == 1, y_near[:, t, :], y_rows[t][:].indirect(n1_t[:, lcols]))
+                fetch(half == 0 and t < 2, y_near[:, t, :], y_rows[t][:].indirect(n1_t[:, lcols]))
             for t in range(PACK):
                 nc.vector.tensor_tensor(y_sum[:, t, :], y_near[:, t, :], y_rows[t][:, cols], ALU.add)
             y_sums.append(y_sum)
@@ -154,6 +154,7 @@ def tile_picked_twhtriebgspan_none_p_kernel(
             return quantise("w3_%d" % n, grouped.rearrange("p n j -> p (n j)"), P)
 
         w3_first = keep.tile([P, P, PACK], BF16, name="w3_first", align_bytes=64)
+        w3_q = [quantise_w3(0, w3_first[:])]
         z_codes = keep.tile([P, S], U32, name="z_codes", align_bytes=64)
         z_scales = keep.tile([P, S], U8, name="z_scales", align_bytes=64)
         for half in range(2):
@@ -163,7 +164,7 @@ def tile_picked_twhtriebgspan_none_p_kernel(
             d_sum = keep.tile([P, PACK, HALF], F32, name="d_sum%d" % half, align_bytes=64)
             gate = work.tile([P, PACK, HALF], F32, name="gate")
             for t in range(PACK):
-                fetch(half == 0 and t < 2, d_near[:, t, :], d_rows[t][:].indirect(n2_t[:, lcols]))
+                fetch(half == 0 or t < 2, d_near[:, t, :], d_rows[t][:].indirect(n2_t[:, lcols]))
             for t in range(PACK):
                 nc.vector.tensor_tensor(d_sum[:, t, :], d_near[:, t, :], d_rows[t][:, cols], ALU.add)
             for pair in range(2):
@@ -179,52 +180,49 @@ def tile_picked_twhtriebgspan_none_p_kernel(
             nc.vector.quantize_mx(
                 out=z_codes[:, cols].bitcast(FP8X4), scales=z_scales[:, cols], in_=z[:].rearrange("p c t -> p (c t)")
             )
-            if half == 0:
-                w3_q = quantise_w3(0, w3_first[:])
-            acc = product(w3_q, 0, z_codes[:, cols], z_scales[:, cols], HALF)
+            acc = product(w3_q[0], 0, z_codes[:, cols], z_scales[:, cols], HALF, "bank%d" % half)
             nc.scalar.copy(h_rows[0][:, cols], acc[:])
 
         w3_rest = keep.tile([P, N - P, PACK], BF16, name="d_sum1", align_bytes=64)
         for n in range(1, N // P):
-            w3_q = quantise_w3(n, w3_rest[:, (n - 1) * P : n * P, :])
-            acc = product(w3_q, 0, z_codes[:], z_scales[:], S)
-            nc.vector.tensor_copy(h_rows[n][:, :S], acc[:])
+            w3_q.append(quantise_w3(n, w3_rest[:, (n - 1) * P : n * P, :]))
 
-        chunks = []
-        for n in range(N // P):
-            widths = [1024, 1024] if n < N // P - 1 else [1024, 512, 512]
-            start = 0
-            for width in widths:
-                chunks.append((n, start, width))
-                start = start + width
-
-        def finish(n, start, width, largest, smallest):
-            places = width // MEMBERS
-            result = pool3.tile([P, places], F32, name="result")
+        def finish(n, first, places, largest, smallest):
+            result = work.tile([P, places], F32, name="result")
             nc.vector.scalar_tensor_tensor(result[:], smallest[:], -0.5, largest[:], ALU.mult, ALU.add)
-            first = start // MEMBERS
             nc.sync.dma_start(out[n * P : (n + 1) * P, first : first + places], result[:])
 
         pending = None
-        for n, start, width in chunks:
-            places = width // MEMBERS
-            members = pool3.tile([P, width], F32, name="members")
-            for s in range(0, width, GATHER):
-                looked_up = h_rows[n][:].indirect(n3_t[:, (start + s) // 16 : (start + s + GATHER) // 16])
-                if n == 0 and start + s == GATHER:
-                    nc.vector.tensor_copy(members[:, s : s + GATHER], looked_up)
+        for n in range(N // P):
+            if n + 1 < N // P:
+                acc = product(w3_q[n + 1], 0, z_codes[:], z_scales[:], S, "bank1")
+                if n == 0:
+                    nc.scalar.copy(h_rows[n + 1][:, :S], acc[:])
                 else:
-                    nc.scalar.activation(members[:, s : s + GATHER], looked_up, ACT.Copy)
-            by_place = members[:].rearrange("p (j m) -> p j m", m=MEMBERS)
-            high = work.tile([P, places, 2], F32, name="high")
-            low = work.tile([P, places, 2], F32, name="low")
-            nc.vector.tensor_tensor(high[:], by_place[:, :, 0:2], by_place[:, :, 2:4], ALU.max)
-            nc.vector.tensor_tensor(low[:], by_place[:, :, 0:2], by_place[:, :, 2:4], ALU.min)
-            if pending is not None:
-                finish(*pending)
-            largest = work.tile([P, places], F32, name="largest")
-            smallest = work.tile([P, places], F32, name="smallest")
-            nc.vector.tensor_tensor(largest[:], high[:, :, 0], high[:, :, 1], ALU.max)
-            nc.vector.tensor_tensor(smallest[:], low[:, :, 0], low[:, :, 1], ALU.min)
-            pending = (n, start, width, largest, smallest)
+                    nc.vector.tensor_copy(h_rows[n + 1][:, :S], acc[:])
+            groups = [[1024, 1024]] if n + 1 < N // P else [[1024, 512], [512]]
+            start = 0
+            for group in groups:
+                places = sum(group) // MEMBERS
+                first = start // MEMBERS
+                high = work.tile([P, places, 2], F32, name="high")
+                low = work.tile([P, places, 2], F32, name="low")
+                for width in group:
+                    members = pool3.tile([P, width], F32, name="members")
+                    for s in range(0, width, GATHER):
+                        looked_up = h_rows[n][:].indirect(n3_t[:, (start + s) // 16 : (start + s + GATHER) // 16])
+                        fetch(n == 0 and s > 0, members[:, s : s + GATHER], looked_up)
+                    by_place = members[:].rearrange("p (j m) -> p j m", m=MEMBERS)
+                    js = slice(start // MEMBERS - first, (start + width) // MEMBERS - first)
+                    nc.vector.tensor_tensor(high[:, js, :], by_place[:, :, 0:2], by_place[:, :, 2:4], ALU.max)
+                    nc.vector.tensor_tensor(low[:, js, :], by_place[:, :, 0:2], by_place[:, :, 2:4], ALU.min)
+                    start = start + width
+                    if pending is not None:
+                        finish(*pending)
+                        pending = None
+                largest = work.tile([P, places], F32, name="largest")
+                smallest = work.tile([P, places], F32, name="smallest")
+                nc.vector.tensor_tensor(largest[:], high[:, :, 0], high[:, :, 1], ALU.max)
+                nc.vector.tensor_tensor(smallest[:], low[:, :, 0], low[:, :, 1], ALU.min)
+                pending = (n, first, places, largest, smallest)
         finish(*pending)

@@ -118,7 +118,10 @@ def tile_picked_twhtriebgspan_none_p_kernel(
             nc.scalar.activation(row[:], acc[:], ACT.Copy, scale=gain[:, t : t + 1])
             y_rows.append(row)
 
-        nc.vector.tensor_copy(*dealt_views(w2_dealt[:, :, P // 2 :, :], w2_raw[1]))
+        nc.vector.tensor_copy(
+            w2_dealt[:, :, P // 2 :, :].rearrange("p (u e) m j -> p u m j e", e=2),
+            w2_raw[1][:].rearrange("p j (m u e) -> p u m j e", u=2, e=2),
+        )
         w2_q = quantise("w2", w2_dealt[:].rearrange("p t m j -> p (t m j)"), H)
 
         d_rows = []
@@ -157,10 +160,11 @@ def tile_picked_twhtriebgspan_none_p_kernel(
         w3_q = [quantise_w3(0, w3_first[:])]
         z_codes = keep.tile([P, S], U32, name="z_codes", align_bytes=64)
         z_scales = keep.tile([P, S], U8, name="z_scales", align_bytes=64)
+        gates = []
         for half in range(2):
             cols = slice(half * HALF, (half + 1) * HALF)
             lcols = slice(half * HALF // 16, (half + 1) * HALF // 16)
-            d_near = work.tile([P, PACK, HALF], F32, name="d_near")
+            d_near = keep.tile([P, PACK, HALF], F32, name="d_near%d" % half, align_bytes=64)
             d_sum = keep.tile([P, PACK, HALF], F32, name="d_sum%d" % half, align_bytes=64)
             gate = work.tile([P, PACK, HALF], F32, name="gate")
             for t in range(PACK):
@@ -170,7 +174,12 @@ def tile_picked_twhtriebgspan_none_p_kernel(
             for pair in range(2):
                 ts = slice(2 * pair, 2 * pair + 2)
                 nc.scalar.activation(gate[:, ts, :], d_sum[:, ts, :], ACT.Sigmoid)
-            z = work.tile([P, HALF, PACK], BF16, name="z", align_bytes=64)
+            gates.append(gate)
+
+        for half in range(2):
+            cols = slice(half * HALF, (half + 1) * HALF)
+            gate = gates[half]
+            z = keep.tile([P, HALF, PACK], BF16, name="d_near%d" % (1 - half), align_bytes=64)
             nc.vector.tensor_tensor(
                 z[:].rearrange("p (c i) t -> p c t i", i=2),
                 y_sums[half][:].rearrange("p t (c i) -> p c t i", i=2),
@@ -205,24 +214,31 @@ def tile_picked_twhtriebgspan_none_p_kernel(
             for group in groups:
                 places = sum(group) // MEMBERS
                 first = start // MEMBERS
-                high = work.tile([P, places, 2], F32, name="high")
-                low = work.tile([P, places, 2], F32, name="low")
+                high = work.tile([P, places // 2, 2, 2], F32, name="high")
+                low = work.tile([P, places // 2, 2, 2], F32, name="low")
                 for width in group:
                     members = pool3.tile([P, width], F32, name="members")
                     for s in range(0, width, GATHER):
                         looked_up = h_rows[n][:].indirect(n3_t[:, (start + s) // 16 : (start + s + GATHER) // 16])
                         fetch(n == 0 and s > 0, members[:, s : s + GATHER], looked_up)
-                    by_place = members[:].rearrange("p (j m) -> p j m", m=MEMBERS)
-                    js = slice(start // MEMBERS - first, (start + width) // MEMBERS - first)
-                    nc.vector.tensor_tensor(high[:, js, :], by_place[:, :, 0:2], by_place[:, :, 2:4], ALU.max)
-                    nc.vector.tensor_tensor(low[:, js, :], by_place[:, :, 0:2], by_place[:, :, 2:4], ALU.min)
+                    by_place = members[:].rearrange("p (a b m) -> p a b m", b=2, m=MEMBERS)
+                    js = slice((start // MEMBERS - first) // 2, ((start + width) // MEMBERS - first) // 2)
+                    for dst, op in ((high, ALU.max), (low, ALU.min)):
+                        nc.vector.tensor_tensor(
+                            dst[:, js, :, :].rearrange("p a e b -> p a b e"),
+                            by_place[:, :, :, 0:2],
+                            by_place[:, :, :, 2:4],
+                            op,
+                        )
                     start = start + width
                     if pending is not None:
                         finish(*pending)
                         pending = None
                 largest = work.tile([P, places], F32, name="largest")
                 smallest = work.tile([P, places], F32, name="smallest")
-                nc.vector.tensor_tensor(largest[:], high[:, :, 0], high[:, :, 1], ALU.max)
-                nc.vector.tensor_tensor(smallest[:], low[:, :, 0], low[:, :, 1], ALU.min)
+                for dst, src, op in ((largest, high, ALU.max), (smallest, low, ALU.min)):
+                    nc.vector.tensor_tensor(
+                        dst[:].rearrange("p (a b) -> p a b", b=2), src[:, :, 0, :], src[:, :, 1, :], op
+                    )
                 pending = (n, first, places, largest, smallest)
         finish(*pending)

from contextlib import ExitStack

import concourse.mybir as mybir

K, T, S, N, H, W = 512, 2048, 512, 512, 512, 2048
FLOPS = 2 * (K * H * S * 2 + H * N * S)

F32 = mybir.dt.float32
BF16 = mybir.dt.bfloat16
I32 = mybir.dt.int32
U32 = mybir.dt.uint32
U16 = mybir.dt.uint16
U8 = mybir.dt.uint8
FP8X4 = mybir.dt.float8_e4m3fn_x4
ALU = mybir.AluOpType
ACT = mybir.ActivationFunctionType

P = 128
PACK = 4
HALF = S // 2
MEMBERS = 4
SPARE = 16
GATHER = 512


def tile_picked_twhtriebgspan_none_p_kernel(
    tc, x_words, x_scales, w1, w2, gn, w3, offs, hz, n1, n2, n3, out
):
    nc = tc.nc
    with ExitStack() as ctx:
        keep = ctx.enter_context(tc.tile_pool(name="keep", bufs=1))
        work = ctx.enter_context(tc.tile_pool(name="work", bufs=2))
        pool3 = ctx.enter_context(tc.tile_pool(name="pool3", bufs=4))
        psum = ctx.enter_context(tc.psum_pool(name="psum", bufs=1))

        offs_t = keep.tile([P, S // 16], U16, name="offs_t")
        hz_t = keep.tile([P, S // 16], U16, name="hz_t")
        n1_t = keep.tile([P, S // 16], U16, name="n1_t")
        n2_t = keep.tile([P, S // 16], U16, name="n2_t")
        n3_t = keep.tile([P, W // 16], U16, name="n3_t")
        word_table = keep.tile([P, T], U32, name="word_table")
        byte_table = keep.tile([P, T], U8, name="byte_table")
        gain = keep.tile([P, PACK], F32, name="gain")
        h_rows = [keep.tile([P, S + SPARE], F32, name="h_rows%d" % n) for n in range(N // P)]

        nc.vector.memset(byte_table[:].bitcast(I32), 0)
        for n in range(N // P):
            nc.gpsimd.memset(h_rows[n][:, S:], 0.0)

        def load_weight(name, w):
            raw = keep.tile([P, PACK, w.shape[1]], F32, name=name)
            nc.sync.dma_start(raw[:], w.rearrange("(p j) c -> p j c", j=PACK))
            return raw

        nc.sync.dma_start(offs_t[:], offs)
        nc.sync.dma_start(hz_t[:], hz)
        nc.sync.dma_start(byte_table[0:P:8, :].bitcast(I32), x_scales[0].bitcast(I32))
        for r in range(1, 4):
            nc.sync.dma_start(byte_table[r:P:32, :].bitcast(I32), x_scales[0][r:16:4, :].bitcast(I32))
        nc.scalar.dma_start(gain[:], gn.rearrange("(p t) o -> p (t o)", t=PACK))
        warm = keep.tile([P, 1], F32, name="warm")
        nc.scalar.activation(warm[:], gain[:, 0:1], ACT.Sigmoid)
        nc.sync.dma_start(word_table[:].bitcast(I32), x_words[0].rearrange("p n t -> p (n t)").bitcast(I32))
        w1_raw = [load_weight("w1_raw%d" % i, w1[:, i * H // 2 : (i + 1) * H // 2]) for i in range(2)]
        w2_raw = [load_weight("w2_raw%d" % i, w2[:, i * H // 2 : (i + 1) * H // 2]) for i in range(2)]

        x_bytes = keep.tile([P, S], U8, name="x_bytes", align_bytes=64)
        nc.vector.tensor_copy(x_bytes[:], byte_table[:].indirect(offs_t[:]))
        hz_picked = keep.tile([P, S], U8, name="hz_picked", align_bytes=64)
        nc.vector.tensor_copy(hz_picked[:], byte_table[:].indirect(hz_t[:]))
        hz_bytes = keep.tile([P, S], U8, name="hz_bytes", align_bytes=64)
        nc.vector.tensor_copy(hz_bytes[:].bitcast(I32), hz_picked[:].bitcast(I32))
        for r in (2, 3):
            nc.sync.dma_start(hz_bytes[r:P:32, :].bitcast(I32), hz_picked[8 * r : P : 32, :].bitcast(I32))
        nc.sync.dma_start(n1_t[:], n1)
        nc.sync.dma_start(n2_t[:], n2)
        w3_raw = load_weight("w3_raw", w3)
        nc.sync.dma_start(n3_t[:], n3)

        def dealt_views(grouped, raw):
            return grouped.rearrange("p t m j -> p m j t"), raw[:].rearrange("p j (m t) -> p m j t", t=PACK)

        def quantise(name, grouped, width):
            codes = keep.tile([P, width], U32, name=name + "_codes", align_bytes=64)
            scales = keep.tile([P, width], U8, name=name + "_scales", align_bytes=64)
            nc.vector.quantize_mx(out=codes[:].bitcast(FP8X4), scales=scales[:], in_=grouped)
            return codes, scales

        def product(weights, block, codes, scales, width, bank):
            acc = psum.tile([P, width], F32, name=bank)
            cols = slice(block * P, (block + 1) * P)
            nc.tensor.matmul_mx(
                out=acc[:],
                lhsT=weights[0][:, cols].bitcast(FP8X4),
                lhsT_scale=weights[1][:, cols],
                rhs=codes.bitcast(FP8X4),
                rhs_scale=scales,
                start=True,
                stop=True,
            )
            return acc

        w1_dealt = keep.tile([P, PACK, P, PACK], BF16, name="w1_dealt", align_bytes=64)
        w2_dealt = keep.tile([P, PACK, P, PACK], BF16, name="w2_dealt", align_bytes=64)
        for i in range(2):
            nc.scalar.copy(*dealt_views(w1_dealt[:, :, i * P // 2 : (i + 1) * P // 2, :], w1_raw[i]))
        x_codes = keep.tile([P, S], U32, name="x_codes", align_bytes=64)
        nc.vector.tensor_copy(x_codes[:], word_table[:].indirect(offs_t[:]))
        hz_codes = keep.tile([P, S], U32, name="hz_codes", align_bytes=64)
        nc.vector.tensor_copy(hz_codes[:], word_table[:].indirect(hz_t[:]))
        w1_q = quantise("w1", w1_dealt[:].rearrange("p t m j -> p (t m j)"), H)
        nc.scalar.copy(*dealt_views(w2_dealt[:, :, : P // 2, :], w2_raw[0]))

        y_rows = []
        for t in range(PACK):
            acc = product(w1_q, t, x_codes[:], x_bytes[:], S, "bank%d" % t)
            row = keep.tile([P, S], F32, name="y_rows%d" % t)
            nc.scalar.activation(row[:], acc[:], ACT.Copy, scale=gain[:, t : t + 1])
            y_rows.append(row)

        nc.vector.tensor_copy(
            w2_dealt[:, :, P // 2 :, :].rearrange("p (u e) m j -> p u m j e", e=2),
            w2_raw[1][:].rearrange("p j (m u e) -> p u m j e", u=2, e=2),
        )
        w2_q = quantise("w2", w2_dealt[:].rearrange("p t m j -> p (t m j)"), H)

        d_rows = []
        for t in range(PACK):
            acc = product(w2_q, t, hz_codes[:], hz_bytes[:], S, "bank%d" % (PACK + t))
            row = keep.tile([P, S], F32, name="d_rows%d" % t)
            nc.scalar.copy(row[:], acc[:])
            d_rows.append(row)

        def fetch(on_vector, dst, looked_up):
            if on_vector:
                nc.vector.tensor_copy(dst, looked_up)
            else:
                nc.scalar.activation(dst, looked_up, ACT.Copy)

        y_sums = []
        for half in range(2):
            cols = slice(half * HALF, (half + 1) * HALF)
            lcols = slice(half * HALF // 16, (half + 1) * HALF // 16)
            y_near = work.tile([P, PACK, HALF], F32, name="y_near")
            y_sum = work.tile([P, PACK, HALF], F32, name="y_sum")
            for t in range(PACK):
                fetch(half == 0 and t < 2, y_near[:, t, :], y_rows[t][:].indirect(n1_t[:, lcols]))
            for t in range(PACK):
                nc.vector.tensor_tensor(y_sum[:, t, :], y_near[:, t, :], y_rows[t][:, cols], ALU.add)
            y_sums.append(y_sum)

        def quantise_w3(n, grouped):
            nc.scalar.copy(
                grouped.rearrange("p (c i) j -> p c j i", i=4),
                w3_raw[:, :, n * P : (n + 1) * P].rearrange("p j (c i) -> p c j i", i=4),
            )
            return quantise("w3_%d" % n, grouped.rearrange("p n j -> p (n j)"), P)

        w3_first = keep.tile([P, P, PACK], BF16, name="w3_first", align_bytes=64)
        w3_q = [quantise_w3(0, w3_first[:])]
        z_codes = keep.tile([P, S], U32, name="z_codes", align_bytes=64)
        z_scales = keep.tile([P, S], U8, name="z_scales", align_bytes=64)
        gates = []
        for half in range(2):
            cols = slice(half * HALF, (half + 1) * HALF)
            lcols = slice(half * HALF // 16, (half + 1) * HALF // 16)
            d_near = keep.tile([P, PACK, HALF], F32, name="d_near%d" % half, align_bytes=64)
            d_sum = keep.tile([P, PACK, HALF], F32, name="d_sum%d" % half, align_bytes=64)
            gate = work.tile([P, PACK, HALF], F32, name="gate")
            for t in range(PACK):
                fetch(half == 0 or t < 2, d_near[:, t, :], d_rows[t][:].indirect(n2_t[:, lcols]))
            for t in range(PACK):
                nc.vector.tensor_tensor(d_sum[:, t, :], d_near[:, t, :], d_rows[t][:, cols], ALU.add)
            for pair in range(2):
                ts = slice(2 * pair, 2 * pair + 2)
                nc.scalar.activation(gate[:, ts, :], d_sum[:, ts, :], ACT.Sigmoid)
            gates.append(gate)

        for half in range(2):
            cols = slice(half * HALF, (half + 1) * HALF)
            gate = gates[half]
            z = keep.tile([P, HALF, PACK], BF16, name="d_near%d" % (1 - half), align_bytes=64)
            nc.vector.tensor_tensor(
                z[:].rearrange("p (c i) t -> p c t i", i=2),
                y_sums[half][:].rearrange("p t (c i) -> p c t i", i=2),
                gate[:].rearrange("p t (c i) -> p c t i", i=2),
                ALU.mult,
            )
            nc.vector.quantize_mx(
                out=z_codes[:, cols].bitcast(FP8X4), scales=z_scales[:, cols], in_=z[:].rearrange("p c t -> p (c t)")
            )
            acc = product(w3_q[0], 0, z_codes[:, cols], z_scales[:, cols], HALF, "bank%d" % half)
            nc.scalar.copy(h_rows[0][:, cols], acc[:])

        w3_rest = keep.tile([P, N - P, PACK], BF16, name="d_sum1", align_bytes=64)
        for n in range(1, N // P):
            w3_q.append(quantise_w3(n, w3_rest[:, (n - 1) * P : n * P, :]))

        def finish(n, first, places, largest, smallest):
            result = work.tile([P, places], F32, name="result")
            nc.vector.scalar_tensor_tensor(result[:], smallest[:], -0.5, largest[:], ALU.mult, ALU.add)
            nc.sync.dma_start(out[n * P : (n + 1) * P, first : first + places], result[:])

        pending = None
        for n in range(N // P):
            if n + 1 < N // P:
                acc = product(w3_q[n + 1], 0, z_codes[:], z_scales[:], S, "bank1")
                if n == 0:
                    nc.scalar.copy(h_rows[n + 1][:, :S], acc[:])
                else:
                    nc.vector.tensor_copy(h_rows[n + 1][:, :S], acc[:])
            groups = [[1024, 1024]] if n + 1 < N // P else [[1024, 512], [512]]
            start = 0
            for group in groups:
                places = sum(group) // MEMBERS
                first = start // MEMBERS
                high = work.tile([P, places // 2, 2, 2], F32, name="high")
                low = work.tile([P, places // 2, 2, 2], F32, name="low")
                for width in group:
                    members = pool3.tile([P, width], F32, name="members")
                    for s in range(0, width, GATHER):
                        looked_up = h_rows[n][:].indirect(n3_t[:, (start + s) // 16 : (start + s + GATHER) // 16])
                        fetch(n == 0 and s > 0, members[:, s : s + GATHER], looked_up)
                    by_place = members[:].rearrange("p (a b m) -> p a b m", b=2, m=MEMBERS)
                    js = slice((start // MEMBERS - first) // 2, ((start + width) // MEMBERS - first) // 2)
                    for dst, op in ((high, ALU.max), (low, ALU.min)):
                        nc.vector.tensor_tensor(
                            dst[:, js, :, :].rearrange("p a e b -> p a b e"),
                            by_place[:, :, :, 0:2],
                            by_place[:, :, :, 2:4],
                            op,
                        )
                    start = start + width
                    if pending is not None:
                        finish(*pending)
                        pending = None
                largest = work.tile([P, places], F32, name="largest")
                smallest = work.tile([P, places], F32, name="smallest")
                for dst, src, op in ((largest, high, ALU.max), (smallest, low, ALU.min)):
                    nc.vector.tensor_tensor(
                        dst[:].rearrange("p (a b) -> p a b", b=2), src[:, :, 0, :], src[:, :, 1, :], op
                    )
                pending = (n, first, places, largest, smallest)
        finish(*pending)
